import numpy as np
import ml_dtypes


def mxq(x, axis, fmt="e4m3"):
    dtype, down = {"e4m3": (ml_dtypes.float8_e4m3fn, 7), "e5m2": (ml_dtypes.float8_e5m2, 14)}[fmt]
    v = np.moveaxis(np.asarray(x, np.float32).astype(ml_dtypes.bfloat16).astype(np.float64), axis, -1)
    blocks = v.reshape(v.shape[:-1] + (-1, 32))
    amax = np.abs(blocks).max(-1, keepdims=True)
    byte = np.maximum(np.where(amax > 0, np.frexp(amax)[1] - 1 + 127, 0) - down, 1)
    scale = np.exp2(byte - 127.0)
    codes = (blocks / scale).astype(np.float32).astype(dtype).astype(np.float64)
    return np.moveaxis((codes * scale).reshape(v.shape), -1, axis)


WIDE = False


def mx_kscale(k):
    if not WIDE:
        return np.ones(k)
    levels = np.array([10, -10, 5, -5, 0])
    if k % 512:
        return np.exp2(np.random.permutation(np.resize(levels, k // 32))).repeat(32)
    a = np.empty((k // 512, 16))
    for p in range(k // 512):
        a[p, :8] = np.random.permutation(np.resize(levels, 8))
        for g in range(8):
            far = levels[np.abs(levels - a[p, g]) >= 10]
            a[p, g + 8] = far[np.random.randint(len(far))]
    return np.exp2(a.ravel()).repeat(32)


def f64(x):
    return np.asarray(x).astype(np.float64)


def striped(idx):
    return np.tile(idx.reshape(-1, 16).T, (8, 1)).astype(np.uint16)


def unstriped(offs):
    return offs[:16].T.reshape(-1).astype(np.int64)


def silu(v):
    return v / (1.0 + np.exp(-np.maximum(v, -700.0)))


K, T, E, C, H, N = 1024, 640, 8, 128, 512, 128
TOP = 4
PAD = 64


def by_expert(wq, xq):
    return np.concatenate([wq[e].T @ xq[:, e * C:(e + 1) * C] for e in range(E)], axis=1)


def setup_inputs():
    n = np.random.standard_normal
    s = mx_kscale(K)[:, None]
    u = mx_kscale(H)
    slot_token = np.empty(E * C, np.int64); pos = np.tile(E * C + np.arange(T) % PAD, (TOP, 1)); taken = np.zeros(T, np.int64)
    liked = np.random.randn(T)
    for e in np.random.permutation(E):
        free = np.flatnonzero(taken < TOP); pick = np.random.permutation(free[np.argsort(-(liked[free] + np.random.gumbel(size=free.size)))[:C]]); slot_token[e * C:(e + 1) * C] = pick
        pos[taken[pick], pick] = e * C + np.arange(C); taken[pick] += 1
    g = np.random.uniform(0.2, 0.8, (TOP, T))
    return {
        "xT": (n((K, T)) * s).astype(np.float32),
        "w1": (n((E, K, H)) / np.sqrt(K) / s[None]).astype(np.float32),
        "w3": (n((E, K, H)) / np.sqrt(K) / s[None] * u[None, None, :]).astype(np.float32),
        "w2": (n((E, H, N)) / np.sqrt(H) / u[None, :, None]).astype(np.float32),
        "gate": np.stack([np.tile(r, (N, 1)) for r in g]).astype(np.float32),
        "offs": striped(slot_token),
        "pos1": striped(pos[0]),
        "pos2": striped(pos[1]),
        "pos3": striped(pos[2]),
        "pos4": striped(pos[3]),
    }


def reference(xT, w1, w3, w2, gate, offs, pos1, pos2, pos3, pos4):
    idx = unstriped(offs)
    xq = mxq(f64(xT)[:, idx], 0, "e4m3")
    h = silu(by_expert(mxq(f64(w1), 1, "e4m3"), xq))
    h = h * by_expert(mxq(f64(w3), 1, "e4m3"), xq)
    y = by_expert(mxq(f64(w2), 1, "e4m3"), mxq(h, 0, "e4m3"))
    y = np.concatenate([y, np.zeros((N, PAD))], axis=1)
    return sum(f64(gate[r]) * y[:, unstriped(p)] for r, p in enumerate((pos1, pos2, pos3, pos4)))

@@ -1,0 +1,287 @@
+from contextlib import ExitStack
+
+import concourse.mybir as mybir
+
+K, T, E, C, H, N = 1024, 640, 8, 128, 512, 128
+TOP = 4
+PAD = 64
+SLOTS = E * C
+FLOPS = 2 * SLOTS * (2 * K * H + H * N)
+
+F32 = mybir.dt.float32
+BF16 = mybir.dt.bfloat16
+U32 = mybir.dt.uint32
+U16 = mybir.dt.uint16
+U8 = mybir.dt.uint8
+FP8X4 = mybir.dt.float8_e4m3fn_x4
+MULT = mybir.AluOpType.mult
+ADD = mybir.AluOpType.add
+SILU = mybir.ActivationFunctionType.Silu
+
+P = 128
+PACK = 4
+K_PASS = P * PACK
+PASSES = K // K_PASS
+LIST_ROWS = 16
+GATHER_EXPERTS = 2
+EARLY = 4
+SHARE = 64
+LAST_SHARE = 48
+RAW_BUFS = 8
+
+
+def tile_moe_ecr_glu_silu_kernel(
+    tc, xT, w1, w3, w2, gate, offs, pos1, pos2, pos3, pos4, out
+):
+    nc = tc.nc
+    with ExitStack() as ctx:
+        lists = ctx.enter_context(tc.tile_pool(name="lists", bufs=1))
+        keep = ctx.enter_context(tc.tile_pool(name="keep", bufs=1))
+        raw = ctx.enter_context(tc.tile_pool(name="raw", bufs=RAW_BUFS))
+        stage = ctx.enter_context(tc.tile_pool(name="stage", bufs=5))
+        codes = ctx.enter_context(tc.tile_pool(name="codes", bufs=6))
+        small = ctx.enter_context(tc.tile_pool(name="small", bufs=2))
+        psum = ctx.enter_context(tc.psum_pool(name="psum", bufs=2))
+
+        def cast(on_scalar, dst, src):
+            if on_scalar:
+                nc.scalar.copy(out=dst, in_=src)
+            else:
+                nc.vector.tensor_copy(out=dst, in_=src)
+
+        def load(view, shape):
+            tile = raw.tile(shape, F32, name="raw", tag="raw")
+            nc.sync.dma_start(out=tile[:], in_=view)
+            return tile
+
+        x_raw = [
+            load(xT[s * K_PASS : (s + 1) * K_PASS, :].rearrange("(p j) t -> p j t", j=PACK), [P, PACK, T])
+            for s in range(PASSES)
+        ]
+        offs_sb = lists.tile([P, SLOTS // LIST_ROWS], U16, name="offs_sb")
+        nc.sync.dma_start(offs_sb[:], offs)
+
+        x_scales = keep.tile([P, T], U8, name="x_scales", align_bytes=64)
+        nc.gpsimd.memset(x_scales[:], 0)
+        y_sb = keep.tile([P, SLOTS + PAD], F32, name="y_sb")
+        nc.gpsimd.memset(y_sb[:, SLOTS:], 0.0)
+
+        x_codes = []
+        for s in range(PASSES):
+            x_bf = stage.tile([P, T * PACK], BF16, name="x_bf", tag="bf", align_bytes=64)
+            cast(
+                s == 0,
+                x_bf[:].rearrange("p (c i j) -> p c j i", i=4, j=PACK),
+                x_raw[s][:].rearrange("p j (c i) -> p c j i", i=4),
+            )
+            words = keep.tile([P, T], U32, name=f"x_codes{s}", align_bytes=64)
+            for lo, hi in ((0, 512), (512, T)):
+                nc.vector.quantize_mx(
+                    out=words[:, lo:hi].bitcast(FP8X4),
+                    scales=x_scales[PACK * s :, lo:hi],
+                    in_=x_bf[:, PACK * lo : PACK * hi],
+                )
+            x_codes.append(words)
+
+        def gather_tokens(first):
+            width = GATHER_EXPERTS * C
+            cols = offs_sb[:, first * C // LIST_ROWS : (first * C + width) // LIST_ROWS]
+            words = []
+            for s in range(PASSES):
+                g = small.tile([P, width], U32, name=f"slot_codes{s}", align_bytes=64)
+                nc.vector.tensor_copy(out=g[:], in_=x_codes[s][:].indirect(cols))
+                words.append(g)
+            sc = small.tile([P, width], U8, name="slot_scales", align_bytes=64)
+            nc.vector.tensor_copy(out=sc[:], in_=x_scales[:].indirect(cols))
+            return words, sc
+
+        def quantize(grouped, width, pool, name):
+            words = pool.tile([P, width], U32, name=name + "_codes", align_bytes=64)
+            scales = pool.tile([P, width], U8, name=name + "_scales", align_bytes=64)
+            nc.vector.quantize_mx(out=words[:].bitcast(FP8X4), scales=scales[:], in_=grouped)
+            return words, scales
+
+        def permuted(grouped):
+            return grouped[:].rearrange("p (t m j) -> p m j t", t=PACK, j=PACK)
+
+        def columns(rows):
+            return rows.rearrange("p j (m t) -> p m j t", t=PACK)
+
+        def bf_tile():
+            return stage.tile([P, PACK * H], BF16, name="w_bf", tag="bf", align_bytes=64)
+
+        def cast_shared(rows, share):
+            g = bf_tile()
+            nc.scalar.copy(out=permuted(g)[:, :share], in_=columns(rows)[:, :share])
+            nc.vector.tensor_copy(out=permuted(g)[:, share:], in_=columns(rows)[:, share:])
+            return g
+
+        def load_whole(w):
+            tile = load(w.rearrange("(s p j) c -> p s (j c)", s=PASSES, j=PACK), [P, PASSES, PACK * H])
+            return [tile[:, s, :].rearrange("p (j c) -> p j c", j=PACK) for s in range(PASSES)]
+
+        def pass_rows(w, s):
+            return w[s * K_PASS : (s + 1) * K_PASS, :].rearrange("(p j) c -> p j c", j=PACK)
+
+        def load_by_pass(w):
+            return [load(pass_rows(w, s), [P, PACK, H])[:] for s in range(PASSES)]
+
+        def quantize_by_tile(g):
+            words = codes.tile([P, H], U32, name="w_codes", align_bytes=64)
+            scales = codes.tile([P, H], U8, name="w_scales", align_bytes=64)
+            for t in range(PACK):
+                m = slice(t * P, (t + 1) * P)
+                nc.vector.quantize_mx(
+                    out=words[:, m].bitcast(FP8X4), scales=scales[:, m], in_=g[:, t * H : (t + 1) * H]
+                )
+            return words, scales
+
+        def project(weights, slot_words, slot_scales, cols, name):
+            acc = psum.tile([P, PACK, C], F32, name=name)
+            for t in range(PACK):
+                m = slice(t * P, (t + 1) * P)
+                for s in range(PASSES):
+                    words, scales = weights[s]
+                    nc.tensor.matmul_mx(
+                        out=acc[:, t, :],
+                        lhsT=words[:, m].bitcast(FP8X4),
+                        lhsT_scale=scales[:, m],
+                        rhs=slot_words[s][:, cols].bitcast(FP8X4),
+                        rhs_scale=slot_scales[PACK * s :, cols],
+                        start=(s == 0),
+                        stop=(s == PASSES - 1),
+                    )
+            return acc
+
+        def w2_view(first, n):
+            return w2[first : first + n].rearrange("e (p j) n -> p e (j n)", j=PACK)
+
+        def cast_w2(rows, on_scalar):
+            g = stage.tile([P, PACK * N], BF16, name="w2_bf", align_bytes=64)
+            cast(
+                on_scalar,
+                g[:].rearrange("p (c i j) -> p c j i", i=4, j=PACK),
+                rows.rearrange("p (j c i) -> p c j i", i=4, j=PACK),
+            )
+            return g
+
+        def quantize_w2(e, g):
+            w2_q[e] = quantize(g[:], N, keep, f"w2_{e}")
+
+        def silu(a_acc, spent):
+            act = spent.rearrange("p (c t) -> p c t", t=PACK)
+            nc.scalar.activation(out=act, in_=a_acc[:].rearrange("p t c -> p c t"), func=SILU)
+            return act
+
+        def gated(act, b_acc, h_bf):
+            nc.vector.tensor_tensor(
+                out=h_bf[:].rearrange("p (c t) -> p c t", t=PACK),
+                in0=b_acc[:].rearrange("p t c -> p c t"),
+                in1=act,
+                op=MULT,
+            )
+
+        def quantize_h(e, h_bf):
+            h_q[e] = quantize(h_bf[:], C, keep, f"h_{e}")
+
+        def second_layer(e, acc):
+            words, scales = w2_q[e]
+            h_words, h_scales = h_q[e]
+            nc.tensor.matmul_mx(
+                out=acc,
+                lhsT=words[:].bitcast(FP8X4),
+                lhsT_scale=scales[:],
+                rhs=h_words[:].bitcast(FP8X4),
+                rhs_scale=h_scales[:],
+                start=True,
+                stop=True,
+            )
+
+        w2_q = {}
+        h_q = {}
+        pos_sb = []
+        slots = gather_tokens(0)
+        a_prev = b_acc = w2_early = None
+        for e in range(E):
+            last = e == E - 1
+            share = LAST_SHARE if last else SHARE
+            cols = slice((e % GATHER_EXPERTS) * C, (e % GATHER_EXPERTS + 1) * C)
+            rows = load_by_pass(w1[e]) if last else load_whole(w1[e])
+            grouped = [cast_shared(r, share) for r in rows]
+            w1_q = [quantize(g[:], H, codes, "w") for g in grouped]
+            a_acc = project(w1_q, slots[0], slots[1], cols, "a_acc")
+            if e == 0:
+                w2_early = keep.tile([P, EARLY, PACK * N], F32, name="w2_early")
+                nc.sync.dma_start(out=w2_early[:], in_=w2_view(0, EARLY))
+                for r, pos in enumerate((pos1, pos2, pos3, pos4)):
+                    pos_tile = lists.tile([P, T // LIST_ROWS], U16, name=f"pos_sb{r}")
+                    nc.sync.dma_start(pos_tile[:], pos)
+                    pos_sb.append(pos_tile)
+            else:
+                act = silu(a_prev, rows[0 if last else 1][:, 0, :])
+                h_bf = small.tile([P, C * PACK], BF16, name="h_bf", align_bytes=64)
+                gated(act, b_acc, h_bf)
+                quantize_h(e - 1, h_bf)
+                if e - 1 < EARLY:
+                    y_acc = psum.tile([P, C], F32, name="y_acc", tag="y")
+                    second_layer(e - 1, y_acc[:])
+                    nc.scalar.copy(out=y_sb[:, (e - 1) * C : e * C], in_=y_acc[:])
+            a_prev = a_acc
+            if last:
+                break
+            grouped = [cast_shared(r, share) for r in load_whole(w3[e])]
+            w3_q = [quantize(g[:], H, codes, "w") for g in grouped]
+            b_acc = project(w3_q, slots[0], slots[1], cols, "b_acc")
+            if (e + 1) % GATHER_EXPERTS == 0:
+                slots = gather_tokens(e + 1)
+            if e < EARLY:
+                quantize_w2(e, cast_w2(w2_early[:, e, :], True))
+
+        first = quantize(cast_shared(load(pass_rows(w3[E - 1], 0), [P, PACK, H])[:], LAST_SHARE)[:], H, codes, "w")
+        g = bf_tile()
+        halves = []
+        for half in range(2):
+            js = slice(2 * half, 2 * half + 2)
+            tile = load(pass_rows(w3[E - 1], 1)[:, js, :], [P, 2, H])
+            cast(half == 0, permuted(g)[:, :, js, :], columns(tile[:]))
+            halves.append(tile)
+        act = silu(a_acc, halves[0][:, 0, :])
+        b_acc = project([first, quantize_by_tile(g)], slots[0], slots[1], cols, "b_acc")
+        late = []
+        for lo in (4, 6):
+            rows = load(w2_view(lo, 2), [P, 2, PACK * N])
+            late.extend(cast_w2(rows[:, i, :], True) for i in range(2))
+        quantize_w2(4, late[0])
+        quantize_w2(5, late[1])
+        gated(act, b_acc, late[1])
+        quantize_w2(6, late[2])
+        quantize_h(7, late[1])
+        quantize_w2(7, late[3])
+        y_late = psum.tile([P, 3, C], F32, name="y_late", tag="y")
+        for i in range(3):
+            second_layer(4 + i, y_late[:, i, :])
+        nc.scalar.copy(out=y_sb[:, 4 * C : 7 * C], in_=y_late[:].rearrange("p i c -> p (i c)"))
+        y_last = psum.tile([P, C], F32, name="y_last", tag="y")
+        second_layer(7, y_last[:])
+        nc.vector.tensor_copy(out=y_sb[:, 7 * C : 8 * C], in_=y_last[:])
+
+        gates = [load(gate[r], [P, T]) for r in range(TOP)]
+        prods = [keep.tile([P, T], F32, name=f"prod{r}") for r in range(TOP)]
+
+        def weigh(r):
+            nc.vector.tensor_tensor(out=prods[r][:], in0=y_sb[:].indirect(pos_sb[r][:]), in1=gates[r][:], op=MULT)
+
+        sum2 = keep.tile([P, T], F32, name="sum2")
+        weigh(0)
+        weigh(1)
+        weigh(2)
+        nc.vector.tensor_tensor(out=sum2[:], in0=prods[0][:], in1=prods[1][:], op=ADD)
+        weigh(3)
+        token_halves = (slice(0, T // 2), slice(T // 2, T))
+        sum3 = [keep.tile([P, T // 2], F32, name=f"sum3_{i}") for i in range(2)]
+        total = [keep.tile([P, T // 2], F32, name=f"total{i}") for i in range(2)]
+        for i, cols in enumerate(token_halves):
+            nc.vector.tensor_tensor(out=sum3[i][:], in0=sum2[:, cols], in1=prods[2][:, cols], op=ADD)
+        for i, cols in enumerate(token_halves):
+            nc.vector.tensor_tensor(out=total[i][:], in0=sum3[i][:], in1=prods[3][:, cols], op=ADD)
+            nc.sync.dma_start(out=out[:, cols], in_=total[i][:])

@@ -24,10 +24,11 @@ K_PASS = P * PACK
 PASSES = K // K_PASS
 LIST_ROWS = 16
 GATHER_EXPERTS = 2
-EARLY = 4
-SHARE = 64
+EARLY = 5
+SHARE = 56
 LAST_SHARE = 48
-RAW_BUFS = 8
+END_SHARE = 40
+RAW_BUFS = 12
 
 
 def tile_moe_ecr_glu_silu_kernel(
@@ -37,11 +38,13 @@ def tile_moe_ecr_glu_silu_kernel(
     with ExitStack() as ctx:
         lists = ctx.enter_context(tc.tile_pool(name="lists", bufs=1))
         keep = ctx.enter_context(tc.tile_pool(name="keep", bufs=1))
-        raw = ctx.enter_context(tc.tile_pool(name="raw", bufs=RAW_BUFS))
+        raw = ctx.enter_context(tc.tile_pool(name="raw", bufs=1))
         stage = ctx.enter_context(tc.tile_pool(name="stage", bufs=5))
         codes = ctx.enter_context(tc.tile_pool(name="codes", bufs=6))
         small = ctx.enter_context(tc.tile_pool(name="small", bufs=2))
         psum = ctx.enter_context(tc.psum_pool(name="psum", bufs=2))
+
+        ring = []
 
         def cast(on_scalar, dst, src):
             if on_scalar:
@@ -50,9 +53,14 @@ def tile_moe_ecr_glu_silu_kernel(
                 nc.vector.tensor_copy(out=dst, in_=src)
 
         def load(view, shape):
-            tile = raw.tile(shape, F32, name="raw", tag="raw")
+            tag = f"ring{len(ring) % RAW_BUFS}"
+            ring.append(tag)
+            tile = raw.tile(shape, F32, name="raw", tag=tag, align_bytes=64)
             nc.sync.dma_start(out=tile[:], in_=view)
             return tile
+
+        def after_load(back, width):
+            return raw.tile([P, width], BF16, name="heir", tag=ring[-back], align_bytes=64)
 
         x_raw = [
             load(xT[s * K_PASS : (s + 1) * K_PASS, :].rearrange("(p j) t -> p j t", j=PACK), [P, PACK, T])
@@ -116,10 +124,6 @@ def tile_moe_ecr_glu_silu_kernel(
             nc.vector.tensor_copy(out=permuted(g)[:, share:], in_=columns(rows)[:, share:])
             return g
 
-        def load_whole(w):
-            tile = load(w.rearrange("(s p j) c -> p s (j c)", s=PASSES, j=PACK), [P, PASSES, PACK * H])
-            return [tile[:, s, :].rearrange("p (j c) -> p j c", j=PACK) for s in range(PASSES)]
-
         def pass_rows(w, s):
             return w[s * K_PASS : (s + 1) * K_PASS, :].rearrange("(p j) c -> p j c", j=PACK)
 
@@ -156,17 +160,16 @@ def tile_moe_ecr_glu_silu_kernel(
         def w2_view(first, n):
             return w2[first : first + n].rearrange("e (p j) n -> p e (j n)", j=PACK)
 
-        def cast_w2(rows, on_scalar):
-            g = stage.tile([P, PACK * N], BF16, name="w2_bf", align_bytes=64)
+        def cast_w2(rows, g):
             cast(
-                on_scalar,
-                g[:].rearrange("p (c i j) -> p c j i", i=4, j=PACK),
+                True,
+                g.rearrange("p (c i j) -> p c j i", i=4, j=PACK),
                 rows.rearrange("p (j c i) -> p c j i", i=4, j=PACK),
             )
             return g
 
         def quantize_w2(e, g):
-            w2_q[e] = quantize(g[:], N, keep, f"w2_{e}")
+            w2_q[e] = quantize(g, N, keep, f"w2_{e}")
 
         def silu(a_acc, spent):
             act = spent.rearrange("p (c t) -> p c t", t=PACK)
@@ -175,14 +178,14 @@ def tile_moe_ecr_glu_silu_kernel(
 
         def gated(act, b_acc, h_bf):
             nc.vector.tensor_tensor(
-                out=h_bf[:].rearrange("p (c t) -> p c t", t=PACK),
+                out=h_bf.rearrange("p (c t) -> p c t", t=PACK),
                 in0=b_acc[:].rearrange("p t c -> p c t"),
                 in1=act,
                 op=MULT,
             )
 
         def quantize_h(e, h_bf):
-            h_q[e] = quantize(h_bf[:], C, keep, f"h_{e}")
+            h_q[e] = quantize(h_bf, C, keep, f"h_{e}")
 
         def second_layer(e, acc):
             words, scales = w2_q[e]
@@ -201,66 +204,63 @@ def tile_moe_ecr_glu_silu_kernel(
         h_q = {}
         pos_sb = []
         slots = gather_tokens(0)
-        a_prev = b_acc = w2_early = None
+        act = b_acc = None
+        w2_early = keep.tile([P, EARLY, PACK * N], F32, name="w2_early")
+        nc.sync.dma_start(out=w2_early[:], in_=w2_view(0, EARLY))
         for e in range(E):
             last = e == E - 1
-            share = LAST_SHARE if last else SHARE
             cols = slice((e % GATHER_EXPERTS) * C, (e % GATHER_EXPERTS + 1) * C)
-            rows = load_by_pass(w1[e]) if last else load_whole(w1[e])
-            grouped = [cast_shared(r, share) for r in rows]
-            w1_q = [quantize(g[:], H, codes, "w") for g in grouped]
-            a_acc = project(w1_q, slots[0], slots[1], cols, "a_acc")
+            rows = load_by_pass(w1[e])
+            grouped = [cast_shared(rows[0], LAST_SHARE), cast_shared(rows[1], SHARE)]
+            w1_q = [quantize(grouped[0][:], H, codes, "w")]
             if e == 0:
-                w2_early = keep.tile([P, EARLY, PACK * N], F32, name="w2_early")
-                nc.sync.dma_start(out=w2_early[:], in_=w2_view(0, EARLY))
                 for r, pos in enumerate((pos1, pos2, pos3, pos4)):
                     pos_tile = lists.tile([P, T // LIST_ROWS], U16, name=f"pos_sb{r}")
                     nc.sync.dma_start(pos_tile[:], pos)
                     pos_sb.append(pos_tile)
             else:
-                act = silu(a_prev, rows[0 if last else 1][:, 0, :])
-                h_bf = small.tile([P, C * PACK], BF16, name="h_bf", align_bytes=64)
+                h_bf = grouped[0][:, : C * PACK]
                 gated(act, b_acc, h_bf)
                 quantize_h(e - 1, h_bf)
                 if e - 1 < EARLY:
                     y_acc = psum.tile([P, C], F32, name="y_acc", tag="y")
                     second_layer(e - 1, y_acc[:])
                     nc.scalar.copy(out=y_sb[:, (e - 1) * C : e * C], in_=y_acc[:])
-            a_prev = a_acc
+            w1_q.append(quantize(grouped[1][:], H, codes, "w"))
+            a_acc = project(w1_q, slots[0], slots[1], cols, "a_acc")
             if last:
                 break
-            grouped = [cast_shared(r, share) for r in load_whole(w3[e])]
+            rows = load_by_pass(w3[e])
+            grouped = [cast_shared(r, SHARE) for r in rows]
+            act = silu(a_acc, rows[1][:, 0, :])
             w3_q = [quantize(g[:], H, codes, "w") for g in grouped]
             b_acc = project(w3_q, slots[0], slots[1], cols, "b_acc")
             if (e + 1) % GATHER_EXPERTS == 0:
                 slots = gather_tokens(e + 1)
             if e < EARLY:
-                quantize_w2(e, cast_w2(w2_early[:, e, :], True))
+                w2_bf = stage.tile([P, PACK * N], BF16, name="w2_bf", align_bytes=64)
+                quantize_w2(e, cast_w2(w2_early[:, e, :], w2_bf[:]))
 
-        first = quantize(cast_shared(load(pass_rows(w3[E - 1], 0), [P, PACK, H])[:], LAST_SHARE)[:], H, codes, "w")
-        g = bf_tile()
-        halves = []
-        for half in range(2):
-            js = slice(2 * half, 2 * half + 2)
-            tile = load(pass_rows(w3[E - 1], 1)[:, js, :], [P, 2, H])
-            cast(half == 0, permuted(g)[:, :, js, :], columns(tile[:]))
-            halves.append(tile)
-        act = silu(a_acc, halves[0][:, 0, :])
+        rows = load_by_pass(w3[E - 1])
+        first = quantize(cast_shared(rows[0], LAST_SHARE)[:], H, codes, "w")
+        act = silu(a_acc, rows[0][:, 0, :])
+        g = cast_shared(rows[1], END_SHARE)
         b_acc = project([first, quantize_by_tile(g)], slots[0], slots[1], cols, "b_acc")
-        late = []
-        for lo in (4, 6):
-            rows = load(w2_view(lo, 2), [P, 2, PACK * N])
-            late.extend(cast_w2(rows[:, i, :], True) for i in range(2))
-        quantize_w2(4, late[0])
-        quantize_w2(5, late[1])
+        late_bf = after_load(1, 3 * PACK * N)
+        late = [late_bf[:, i * PACK * N : (i + 1) * PACK * N] for i in range(3)]
+        for lo, n in ((5, 1), (6, 2)):
+            rows = load(w2_view(lo, n), [P, n, PACK * N])
+            for i in range(n):
+                cast_w2(rows[:, i, :], late[lo + i - 5])
+        quantize_w2(5, late[0])
+        quantize_w2(6, late[1])
         gated(act, b_acc, late[1])
-        quantize_w2(6, late[2])
+        quantize_w2(7, late[2])
         quantize_h(7, late[1])
-        quantize_w2(7, late[3])
-        y_late = psum.tile([P, 3, C], F32, name="y_late", tag="y")
-        for i in range(3):
-            second_layer(4 + i, y_late[:, i, :])
-        nc.scalar.copy(out=y_sb[:, 4 * C : 7 * C], in_=y_late[:].rearrange("p i c -> p (i c)"))
+        y_late = psum.tile([P, 2, C], F32, name="y_late", tag="y")
+        for i in range(2):
+            second_layer(5 + i, y_late[:, i, :])
+        nc.scalar.copy(out=y_sb[:, 5 * C : 7 * C], in_=y_late[:].rearrange("p i c -> p (i c)"))
         y_last = psum.tile([P, C], F32, name="y_last", tag="y")
         second_layer(7, y_last[:])
         nc.vector.tensor_copy(out=y_sb[:, 7 * C : 8 * C], in_=y_last[:])

@@ -25,10 +25,12 @@ PASSES = K // K_PASS
 LIST_ROWS = 16
 GATHER_EXPERTS = 2
 EARLY = 5
-SHARE = 56
-LAST_SHARE = 48
-END_SHARE = 40
-RAW_BUFS = 12
+SHARE = 68
+LAST_SHARES = (48, 56, 48, 40)
+PAIRED = 2
+WHOLE = 5
+RAW_BUFS = 4
+BF_BUFS = 2
 
 
 def tile_moe_ecr_glu_silu_kernel(
@@ -39,12 +41,13 @@ def tile_moe_ecr_glu_silu_kernel(
         lists = ctx.enter_context(tc.tile_pool(name="lists", bufs=1))
         keep = ctx.enter_context(tc.tile_pool(name="keep", bufs=1))
         raw = ctx.enter_context(tc.tile_pool(name="raw", bufs=1))
-        stage = ctx.enter_context(tc.tile_pool(name="stage", bufs=5))
+        stage = ctx.enter_context(tc.tile_pool(name="stage", bufs=1))
         codes = ctx.enter_context(tc.tile_pool(name="codes", bufs=6))
         small = ctx.enter_context(tc.tile_pool(name="small", bufs=2))
         psum = ctx.enter_context(tc.psum_pool(name="psum", bufs=2))
 
         ring = []
+        bf_ring = []
 
         def cast(on_scalar, dst, src):
             if on_scalar:
@@ -52,20 +55,18 @@ def tile_moe_ecr_glu_silu_kernel(
             else:
                 nc.vector.tensor_copy(out=dst, in_=src)
 
-        def load(view, shape):
+        def ring_tile(shape):
             tag = f"ring{len(ring) % RAW_BUFS}"
             ring.append(tag)
-            tile = raw.tile(shape, F32, name="raw", tag=tag, align_bytes=64)
-            nc.sync.dma_start(out=tile[:], in_=view)
-            return tile
+            return raw.tile(shape, F32, name="raw", tag=tag, align_bytes=64)
 
-        def after_load(back, width):
-            return raw.tile([P, width], BF16, name="heir", tag=ring[-back], align_bytes=64)
+        def bf_tile(width):
+            tag = f"bf{len(bf_ring) % BF_BUFS}"
+            bf_ring.append(tag)
+            return stage.tile([P, width], BF16, name="bf", tag=tag, align_bytes=64)
 
-        x_raw = [
-            load(xT[s * K_PASS : (s + 1) * K_PASS, :].rearrange("(p j) t -> p j t", j=PACK), [P, PACK, T])
-            for s in range(PASSES)
-        ]
+        x_raw = ring_tile([P, PASSES, PACK * T])
+        nc.sync.dma_start(out=x_raw[:], in_=xT.rearrange("(s p j) t -> p s (j t)", s=PASSES, j=PACK))
         offs_sb = lists.tile([P, SLOTS // LIST_ROWS], U16, name="offs_sb")
         nc.sync.dma_start(offs_sb[:], offs)
 
@@ -76,11 +77,11 @@ def tile_moe_ecr_glu_silu_kernel(
 
         x_codes = []
         for s in range(PASSES):
-            x_bf = stage.tile([P, T * PACK], BF16, name="x_bf", tag="bf", align_bytes=64)
+            x_bf = bf_tile(T * PACK)
             cast(
                 s == 0,
                 x_bf[:].rearrange("p (c i j) -> p c j i", i=4, j=PACK),
-                x_raw[s][:].rearrange("p j (c i) -> p c j i", i=4),
+                x_raw[:, s, :].rearrange("p (j c i) -> p c j i", i=4, j=PACK),
             )
             words = keep.tile([P, T], U32, name=f"x_codes{s}", align_bytes=64)
             for lo, hi in ((0, 512), (512, T)):
@@ -96,10 +97,10 @@ def tile_moe_ecr_glu_silu_kernel(
             cols = offs_sb[:, first * C // LIST_ROWS : (first * C + width) // LIST_ROWS]
             words = []
             for s in range(PASSES):
-                g = small.tile([P, width], U32, name=f"slot_codes{s}", align_bytes=64)
+                g = keep.tile([P, width], U32, name=f"slot_codes{s}_{first}", align_bytes=64)
                 nc.vector.tensor_copy(out=g[:], in_=x_codes[s][:].indirect(cols))
                 words.append(g)
-            sc = small.tile([P, width], U8, name="slot_scales", align_bytes=64)
+            sc = keep.tile([P, width], U8, name=f"slot_scales{first}", align_bytes=64)
             nc.vector.tensor_copy(out=sc[:], in_=x_scales[:].indirect(cols))
             return words, sc
 
@@ -113,22 +114,17 @@ def tile_moe_ecr_glu_silu_kernel(
             return grouped[:].rearrange("p (t m j) -> p m j t", t=PACK, j=PACK)
 
         def columns(rows):
-            return rows.rearrange("p j (m t) -> p m j t", t=PACK)
-
-        def bf_tile():
-            return stage.tile([P, PACK * H], BF16, name="w_bf", tag="bf", align_bytes=64)
+            return rows.rearrange("p (j m t) -> p m j t", t=PACK, j=PACK)
 
         def cast_shared(rows, share):
-            g = bf_tile()
+            g = bf_tile(PACK * H)
             nc.scalar.copy(out=permuted(g)[:, :share], in_=columns(rows)[:, :share])
             nc.vector.tensor_copy(out=permuted(g)[:, share:], in_=columns(rows)[:, share:])
             return g
 
-        def pass_rows(w, s):
-            return w[s * K_PASS : (s + 1) * K_PASS, :].rearrange("(p j) c -> p j c", j=PACK)
-
-        def load_by_pass(w):
-            return [load(pass_rows(w, s), [P, PACK, H])[:] for s in range(PASSES)]
+        def load_passes(dst, w, first, count):
+            rows = w.rearrange("e (s p j) c -> p (e s) (j c)", s=PASSES, j=PACK)
+            nc.sync.dma_start(out=dst, in_=rows[:, first : first + count, :])
 
         def quantize_by_tile(g):
             words = codes.tile([P, H], U32, name="w_codes", align_bytes=64)
@@ -204,52 +200,73 @@ def tile_moe_ecr_glu_silu_kernel(
         h_q = {}
         pos_sb = []
         slots = gather_tokens(0)
-        act = b_acc = None
         w2_early = keep.tile([P, EARLY, PACK * N], F32, name="w2_early")
         nc.sync.dma_start(out=w2_early[:], in_=w2_view(0, EARLY))
-        for e in range(E):
-            last = e == E - 1
-            cols = slice((e % GATHER_EXPERTS) * C, (e % GATHER_EXPERTS + 1) * C)
-            rows = load_by_pass(w1[e])
-            grouped = [cast_shared(rows[0], LAST_SHARE), cast_shared(rows[1], SHARE)]
-            w1_q = [quantize(grouped[0][:], H, codes, "w")]
-            if e == 0:
+        chunks = []
+        for which, w in enumerate((w1, w3)):
+            tile = ring_tile([P, PAIRED * PASSES, PACK * H])
+            load_passes(tile[:], w, 0, PAIRED * PASSES)
+            chunks.extend((which, i // PASSES, i % PASSES, tile[:, i, :]) for i in range(PAIRED * PASSES))
+            if which == 0:
                 for r, pos in enumerate((pos1, pos2, pos3, pos4)):
                     pos_tile = lists.tile([P, T // LIST_ROWS], U16, name=f"pos_sb{r}")
                     nc.sync.dma_start(pos_tile[:], pos)
                     pos_sb.append(pos_tile)
-            else:
-                h_bf = grouped[0][:, : C * PACK]
-                gated(act, b_acc, h_bf)
-                quantize_h(e - 1, h_bf)
-                if e - 1 < EARLY:
-                    y_acc = psum.tile([P, C], F32, name="y_acc", tag="y")
-                    second_layer(e - 1, y_acc[:])
-                    nc.scalar.copy(out=y_sb[:, (e - 1) * C : e * C], in_=y_acc[:])
-            w1_q.append(quantize(grouped[1][:], H, codes, "w"))
-            a_acc = project(w1_q, slots[0], slots[1], cols, "a_acc")
-            if last:
-                break
-            rows = load_by_pass(w3[e])
-            grouped = [cast_shared(r, SHARE) for r in rows]
-            act = silu(a_acc, rows[1][:, 0, :])
-            w3_q = [quantize(g[:], H, codes, "w") for g in grouped]
-            b_acc = project(w3_q, slots[0], slots[1], cols, "b_acc")
-            if (e + 1) % GATHER_EXPERTS == 0:
-                slots = gather_tokens(e + 1)
-            if e < EARLY:
-                w2_bf = stage.tile([P, PACK * N], BF16, name="w2_bf", align_bytes=64)
-                quantize_w2(e, cast_w2(w2_early[:, e, :], w2_bf[:]))
 
-        rows = load_by_pass(w3[E - 1])
-        first = quantize(cast_shared(rows[0], LAST_SHARE)[:], H, codes, "w")
-        act = silu(a_acc, rows[0][:, 0, :])
-        g = cast_shared(rows[1], END_SHARE)
-        b_acc = project([first, quantize_by_tile(g)], slots[0], slots[1], cols, "b_acc")
-        late_bf = after_load(1, 3 * PACK * N)
+        def load_expert(e):
+            count = 2 * PASSES - (1 if e == E - 1 else 0)
+            tile = ring_tile([P, count, PACK * H])
+            step = PASSES if e < WHOLE else 1
+            for i in range(0, count, step):
+                load_passes(tile[:, i : i + step, :], (w1, w3)[i // PASSES], e * PASSES + i % PASSES, step)
+            chunks.extend((i // PASSES, e, i % PASSES, tile[:, i, :]) for i in range(count))
+
+        total_chunks = 2 * PASSES * E
+        w_q, a_acc, slots_of = {}, {}, {0: slots}
+        waiting = []
+        for index in range(total_chunks - 1):
+            if index == len(chunks):
+                load_expert(index // (2 * PASSES))
+            which, e, s, rows = chunks[index]
+            pair = e // GATHER_EXPERTS
+            if pair not in slots_of:
+                slots_of[pair] = gather_tokens(e)
+            left = total_chunks - index
+            g = cast_shared(rows, LAST_SHARES[-left] if left <= len(LAST_SHARES) else SHARE)
+            w_q[which, e, s] = quantize(g[:], H, codes, "w")
+            for done, act, b_acc in waiting:
+                h_bf = g[:, : C * PACK]
+                gated(act, b_acc, h_bf)
+                quantize_h(done, h_bf)
+                if done < EARLY:
+                    w2_bf = small.tile([P, PACK * N], BF16, name="w2_bf", align_bytes=64)
+                    quantize_w2(done, cast_w2(w2_early[:, done, :], w2_bf[:]))
+                if done == 3:
+                    y_acc = psum.tile([P, 4, C], F32, name="y_acc", tag="y")
+                    for i in range(4):
+                        second_layer(i, y_acc[:, i, :])
+                    nc.scalar.copy(out=y_sb[:, : 4 * C], in_=y_acc[:].rearrange("p i c -> p (i c)"))
+            waiting = []
+            cols = slice((e % GATHER_EXPERTS) * C, (e % GATHER_EXPERTS + 1) * C)
+            if s == PASSES - 1:
+                both = [w_q[which, e, 0], w_q[which, e, 1]]
+                acc = project(both, slots_of[pair][0], slots_of[pair][1], cols, ("a_acc", "b_acc")[which])
+                if which == 0:
+                    a_acc[e] = acc
+                else:
+                    waiting = [(e, silu(a_acc[e], rows[:, : C * PACK]), acc)]
+
+        act = silu(a_acc[E - 1], rows[:, : C * PACK])
+        end_raw = ring_tile([P, 1, PACK * H])
+        load_passes(end_raw[:], w3, E * PASSES - 1, 1)
+        g = cast_shared(end_raw[:, 0, :], LAST_SHARES[-1])
+        b_acc = project([w_q[1, E - 1, 0], quantize_by_tile(g)], slots_of[pair][0], slots_of[pair][1], cols, "b_acc")
+        late_bf = raw.tile([P, 3 * PACK * N], BF16, name="late_bf", tag=ring[-1], align_bytes=64)
+        tail = ring_tile([P, 3 * PACK * N + TOP * T])
         late = [late_bf[:, i * PACK * N : (i + 1) * PACK * N] for i in range(3)]
         for lo, n in ((5, 1), (6, 2)):
-            rows = load(w2_view(lo, n), [P, n, PACK * N])
+            rows = tail[:, (lo - 5) * PACK * N : (lo - 5 + n) * PACK * N].rearrange("p (e x) -> p e x", e=n)
+            nc.sync.dma_start(out=rows, in_=w2_view(lo, n))
             for i in range(n):
                 cast_w2(rows[:, i, :], late[lo + i - 5])
         quantize_w2(5, late[0])
@@ -257,19 +274,21 @@ def tile_moe_ecr_glu_silu_kernel(
         gated(act, b_acc, late[1])
         quantize_w2(7, late[2])
         quantize_h(7, late[1])
-        y_late = psum.tile([P, 2, C], F32, name="y_late", tag="y")
-        for i in range(2):
-            second_layer(5 + i, y_late[:, i, :])
-        nc.scalar.copy(out=y_sb[:, 5 * C : 7 * C], in_=y_late[:].rearrange("p i c -> p (i c)"))
+        y_late = psum.tile([P, 3, C], F32, name="y_late", tag="y")
+        for i in range(3):
+            second_layer(4 + i, y_late[:, i, :])
+        nc.scalar.copy(out=y_sb[:, 4 * C : 7 * C], in_=y_late[:].rearrange("p i c -> p (i c)"))
         y_last = psum.tile([P, C], F32, name="y_last", tag="y")
         second_layer(7, y_last[:])
         nc.vector.tensor_copy(out=y_sb[:, 7 * C : 8 * C], in_=y_last[:])
 
-        gates = [load(gate[r], [P, T]) for r in range(TOP)]
+        gates = [tail[:, 3 * PACK * N + r * T : 3 * PACK * N + (r + 1) * T] for r in range(TOP)]
+        for r in range(TOP):
+            nc.sync.dma_start(out=gates[r], in_=gate[r])
         prods = [keep.tile([P, T], F32, name=f"prod{r}") for r in range(TOP)]
 
         def weigh(r):
-            nc.vector.tensor_tensor(out=prods[r][:], in0=y_sb[:].indirect(pos_sb[r][:]), in1=gates[r][:], op=MULT)
+            nc.vector.tensor_tensor(out=prods[r][:], in0=y_sb[:].indirect(pos_sb[r][:]), in1=gates[r], op=MULT)
 
         sum2 = keep.tile([P, T], F32, name="sum2")
         weigh(0)

@@ -24,9 +24,10 @@ K_PASS = P * PACK
 PASSES = K // K_PASS
 LIST_ROWS = 16
 GATHER_EXPERTS = 2
-EARLY = 5
+EARLY = 3
+LATE = E - EARLY
 SHARE = 68
-LAST_SHARES = (48, 56, 48, 40)
+LAST_SHARES = (48, 56, 48)
 PAIRED = 2
 WHOLE = 5
 RAW_BUFS = 4
@@ -60,10 +61,10 @@ def tile_moe_ecr_glu_silu_kernel(
             ring.append(tag)
             return raw.tile(shape, F32, name="raw", tag=tag, align_bytes=64)
 
-        def bf_tile(width):
+        def bf_tile(width, dtype=BF16):
             tag = f"bf{len(bf_ring) % BF_BUFS}"
             bf_ring.append(tag)
-            return stage.tile([P, width], BF16, name="bf", tag=tag, align_bytes=64)
+            return stage.tile([P, width], dtype, name="bf", tag=tag, align_bytes=64)
 
         x_raw = ring_tile([P, PASSES, PACK * T])
         nc.sync.dma_start(out=x_raw[:], in_=xT.rearrange("(s p j) t -> p s (j t)", s=PASSES, j=PACK))
@@ -165,7 +166,8 @@ def tile_moe_ecr_glu_silu_kernel(
             return g
 
         def quantize_w2(e, g):
-            w2_q[e] = quantize(g, N, keep, f"w2_{e}")
+            words, scales = quantize(g, N, keep, f"w2_{e}")
+            w2_q[e] = (words[:], scales[:])
 
         def silu(a_acc, spent):
             act = spent.rearrange("p (c t) -> p c t", t=PACK)
@@ -188,8 +190,8 @@ def tile_moe_ecr_glu_silu_kernel(
             h_words, h_scales = h_q[e]
             nc.tensor.matmul_mx(
                 out=acc,
-                lhsT=words[:].bitcast(FP8X4),
-                lhsT_scale=scales[:],
+                lhsT=words.bitcast(FP8X4),
+                lhsT_scale=scales,
                 rhs=h_words[:].bitcast(FP8X4),
                 rhs_scale=h_scales[:],
                 start=True,
@@ -231,7 +233,7 @@ def tile_moe_ecr_glu_silu_kernel(
             pair = e // GATHER_EXPERTS
             if pair not in slots_of:
                 slots_of[pair] = gather_tokens(e)
-            left = total_chunks - index
+            left = total_chunks - 1 - index
             g = cast_shared(rows, LAST_SHARES[-left] if left <= len(LAST_SHARES) else SHARE)
             w_q[which, e, s] = quantize(g[:], H, codes, "w")
             for done, act, b_acc in waiting:
@@ -241,11 +243,11 @@ def tile_moe_ecr_glu_silu_kernel(
                 if done < EARLY:
                     w2_bf = small.tile([P, PACK * N], BF16, name="w2_bf", align_bytes=64)
                     quantize_w2(done, cast_w2(w2_early[:, done, :], w2_bf[:]))
-                if done == 3:
-                    y_acc = psum.tile([P, 4, C], F32, name="y_acc", tag="y")
-                    for i in range(4):
+                if done == EARLY - 1:
+                    y_acc = psum.tile([P, EARLY, C], F32, name="y_acc", tag="y")
+                    for i in range(EARLY):
                         second_layer(i, y_acc[:, i, :])
-                    nc.scalar.copy(out=y_sb[:, : 4 * C], in_=y_acc[:].rearrange("p i c -> p (i c)"))
+                    nc.scalar.copy(out=y_sb[:, : EARLY * C], in_=y_acc[:].rearrange("p i c -> p (i c)"))
             waiting = []
             cols = slice((e % GATHER_EXPERTS) * C, (e % GATHER_EXPERTS + 1) * C)
             if s == PASSES - 1:
@@ -259,30 +261,39 @@ def tile_moe_ecr_glu_silu_kernel(
         act = silu(a_acc[E - 1], rows[:, : C * PACK])
         end_raw = ring_tile([P, 1, PACK * H])
         load_passes(end_raw[:], w3, E * PASSES - 1, 1)
-        g = cast_shared(end_raw[:, 0, :], LAST_SHARES[-1])
+        g = bf_tile(PACK * H)
+        nc.vector.tensor_copy(out=permuted(g), in_=columns(end_raw[:, 0, :]))
         b_acc = project([w_q[1, E - 1, 0], quantize_by_tile(g)], slots_of[pair][0], slots_of[pair][1], cols, "b_acc")
-        late_bf = raw.tile([P, 3 * PACK * N], BF16, name="late_bf", tag=ring[-1], align_bytes=64)
-        tail = ring_tile([P, 3 * PACK * N + TOP * T])
-        late = [late_bf[:, i * PACK * N : (i + 1) * PACK * N] for i in range(3)]
-        for lo, n in ((5, 1), (6, 2)):
-            rows = tail[:, (lo - 5) * PACK * N : (lo - 5 + n) * PACK * N].rearrange("p (e x) -> p e x", e=n)
-            nc.sync.dma_start(out=rows, in_=w2_view(lo, n))
-            for i in range(n):
-                cast_w2(rows[:, i, :], late[lo + i - 5])
-        quantize_w2(5, late[0])
-        quantize_w2(6, late[1])
-        gated(act, b_acc, late[1])
-        quantize_w2(7, late[2])
-        quantize_h(7, late[1])
-        y_late = psum.tile([P, 3, C], F32, name="y_late", tag="y")
-        for i in range(3):
-            second_layer(4 + i, y_late[:, i, :])
-        nc.scalar.copy(out=y_sb[:, 4 * C : 7 * C], in_=y_late[:].rearrange("p i c -> p (i c)"))
+        late_bf = bf_tile(LATE * PACK * N)
+        late_codes = bf_tile(LATE * N, U32)
+        late_scales = keep.tile([P, LATE * N], U8, name="late_scales", align_bytes=64)
+        tail = ring_tile([P, LATE * PACK * N + TOP * T])
+        late = [late_bf[:, i * PACK * N : (i + 1) * PACK * N] for i in range(LATE)]
+        for i in range(LATE):
+            rows = tail[:, i * PACK * N : (i + 1) * PACK * N]
+            nc.sync.dma_start(out=rows, in_=w2[EARLY + i].rearrange("(p j) n -> p (j n)", j=PACK))
+            cast_w2(rows, late[i])
+
+        def quantize_late(i):
+            words, scales = late_codes[:, i * N : (i + 1) * N], late_scales[:, i * N : (i + 1) * N]
+            nc.vector.quantize_mx(out=words.bitcast(FP8X4), scales=scales, in_=late[i])
+            w2_q[EARLY + i] = (words, scales)
+
+        for i in range(LATE - 2):
+            quantize_late(i)
+        gated(act, b_acc, late[LATE - 3])
+        quantize_late(LATE - 2)
+        quantize_h(E - 1, late[LATE - 3])
+        quantize_late(LATE - 1)
+        y_late = psum.tile([P, LATE - 1, C], F32, name="y_late", tag="y")
+        for i in range(LATE - 1):
+            second_layer(EARLY + i, y_late[:, i, :])
+        nc.scalar.copy(out=y_sb[:, EARLY * C : (E - 1) * C], in_=y_late[:].rearrange("p i c -> p (i c)"))
         y_last = psum.tile([P, C], F32, name="y_last", tag="y")
         second_layer(7, y_last[:])
         nc.vector.tensor_copy(out=y_sb[:, 7 * C : 8 * C], in_=y_last[:])
 
-        gates = [tail[:, 3 * PACK * N + r * T : 3 * PACK * N + (r + 1) * T] for r in range(TOP)]
+        gates = [tail[:, LATE * PACK * N + r * T : LATE * PACK * N + (r + 1) * T] for r in range(TOP)]
         for r in range(TOP):
             nc.sync.dma_start(out=gates[r], in_=gate[r])
         prods = [keep.tile([P, T], F32, name=f"prod{r}") for r in range(TOP)]

from contextlib import ExitStack

import concourse.mybir as mybir

K, T, E, C, H, N = 1024, 640, 8, 128, 512, 128
TOP = 4
PAD = 64
SLOTS = E * C
FLOPS = 2 * SLOTS * (2 * K * H + H * N)

F32 = mybir.dt.float32
BF16 = mybir.dt.bfloat16
U32 = mybir.dt.uint32
U16 = mybir.dt.uint16
U8 = mybir.dt.uint8
FP8X4 = mybir.dt.float8_e4m3fn_x4
MULT = mybir.AluOpType.mult
ADD = mybir.AluOpType.add
SILU = mybir.ActivationFunctionType.Silu

P = 128
PACK = 4
K_PASS = P * PACK
PASSES = K // K_PASS
LIST_ROWS = 16
GATHER_EXPERTS = 2
EARLY = 3
LATE = E - EARLY
SHARE = 68
LAST_SHARES = (48, 56, 48)
PAIRED = 2
WHOLE = 5
RAW_BUFS = 4
BF_BUFS = 2


def tile_moe_ecr_glu_silu_kernel(
    tc, xT, w1, w3, w2, gate, offs, pos1, pos2, pos3, pos4, out
):
    nc = tc.nc
    with ExitStack() as ctx:
        lists = ctx.enter_context(tc.tile_pool(name="lists", bufs=1))
        keep = ctx.enter_context(tc.tile_pool(name="keep", bufs=1))
        raw = ctx.enter_context(tc.tile_pool(name="raw", bufs=1))
        stage = ctx.enter_context(tc.tile_pool(name="stage", bufs=1))
        codes = ctx.enter_context(tc.tile_pool(name="codes", bufs=6))
        small = ctx.enter_context(tc.tile_pool(name="small", bufs=2))
        psum = ctx.enter_context(tc.psum_pool(name="psum", bufs=2))

        ring = []
        bf_ring = []

        def cast(on_scalar, dst, src):
            if on_scalar:
                nc.scalar.copy(out=dst, in_=src)
            else:
                nc.vector.tensor_copy(out=dst, in_=src)

        def ring_tile(shape):
            tag = f"ring{len(ring) % RAW_BUFS}"
            ring.append(tag)
            return raw.tile(shape, F32, name="raw", tag=tag, align_bytes=64)

        def bf_tile(width, dtype=BF16):
            tag = f"bf{len(bf_ring) % BF_BUFS}"
            bf_ring.append(tag)
            return stage.tile([P, width], dtype, name="bf", tag=tag, align_bytes=64)

        x_raw = ring_tile([P, PASSES, PACK * T])
        nc.sync.dma_start(out=x_raw[:], in_=xT.rearrange("(s p j) t -> p s (j t)", s=PASSES, j=PACK))
        offs_sb = lists.tile([P, SLOTS // LIST_ROWS], U16, name="offs_sb")
        nc.sync.dma_start(offs_sb[:], offs)

        x_scales = keep.tile([P, T], U8, name="x_scales", align_bytes=64)
        nc.gpsimd.memset(x_scales[:], 0)
        y_sb = keep.tile([P, SLOTS + PAD], F32, name="y_sb")
        nc.gpsimd.memset(y_sb[:, SLOTS:], 0.0)

        x_codes = []
        for s in range(PASSES):
            x_bf = bf_tile(T * PACK)
            cast(
                s == 0,
                x_bf[:].rearrange("p (c i j) -> p c j i", i=4, j=PACK),
                x_raw[:, s, :].rearrange("p (j c i) -> p c j i", i=4, j=PACK),
            )
            words = keep.tile([P, T], U32, name=f"x_codes{s}", align_bytes=64)
            for lo, hi in ((0, 512), (512, T)):
                nc.vector.quantize_mx(
                    out=words[:, lo:hi].bitcast(FP8X4),
                    scales=x_scales[PACK * s :, lo:hi],
                    in_=x_bf[:, PACK * lo : PACK * hi],
                )
            x_codes.append(words)

        def gather_tokens(first):
            width = GATHER_EXPERTS * C
            cols = offs_sb[:, first * C // LIST_ROWS : (first * C + width) // LIST_ROWS]
            words = []
            for s in range(PASSES):
                g = keep.tile([P, width], U32, name=f"slot_codes{s}_{first}", align_bytes=64)
                nc.vector.tensor_copy(out=g[:], in_=x_codes[s][:].indirect(cols))
                words.append(g)
            sc = keep.tile([P, width], U8, name=f"slot_scales{first}", align_bytes=64)
            nc.vector.tensor_copy(out=sc[:], in_=x_scales[:].indirect(cols))
            return words, sc

        def quantize(grouped, width, pool, name):
            words = pool.tile([P, width], U32, name=name + "_codes", align_bytes=64)
            scales = pool.tile([P, width], U8, name=name + "_scales", align_bytes=64)
            nc.vector.quantize_mx(out=words[:].bitcast(FP8X4), scales=scales[:], in_=grouped)
            return words, scales

        def permuted(grouped):
            return grouped[:].rearrange("p (t m j) -> p m j t", t=PACK, j=PACK)

        def columns(rows):
            return rows.rearrange("p (j m t) -> p m j t", t=PACK, j=PACK)

        def cast_shared(rows, share):
            g = bf_tile(PACK * H)
            nc.scalar.copy(out=permuted(g)[:, :share], in_=columns(rows)[:, :share])
            nc.vector.tensor_copy(out=permuted(g)[:, share:], in_=columns(rows)[:, share:])
            return g

        def load_passes(dst, w, first, count):
            rows = w.rearrange("e (s p j) c -> p (e s) (j c)", s=PASSES, j=PACK)
            nc.sync.dma_start(out=dst, in_=rows[:, first : first + count, :])

        def quantize_by_tile(g):
            words = codes.tile([P, H], U32, name="w_codes", align_bytes=64)
            scales = codes.tile([P, H], U8, name="w_scales", align_bytes=64)
            for t in range(PACK):
                m = slice(t * P, (t + 1) * P)
                nc.vector.quantize_mx(
                    out=words[:, m].bitcast(FP8X4), scales=scales[:, m], in_=g[:, t * H : (t + 1) * H]
                )
            return words, scales

        def project(weights, slot_words, slot_scales, cols, name):
            acc = psum.tile([P, PACK, C], F32, name=name)
            for t in range(PACK):
                m = slice(t * P, (t + 1) * P)
                for s in range(PASSES):
                    words, scales = weights[s]
                    nc.tensor.matmul_mx(
                        out=acc[:, t, :],
                        lhsT=words[:, m].bitcast(FP8X4),
                        lhsT_scale=scales[:, m],
                        rhs=slot_words[s][:, cols].bitcast(FP8X4),
                        rhs_scale=slot_scales[PACK * s :, cols],
                        start=(s == 0),
                        stop=(s == PASSES - 1),
                    )
            return acc

        def w2_view(first, n):
            return w2[first : first + n].rearrange("e (p j) n -> p e (j n)", j=PACK)

        def cast_w2(rows, g):
            cast(
                True,
                g.rearrange("p (c i j) -> p c j i", i=4, j=PACK),
                rows.rearrange("p (j c i) -> p c j i", i=4, j=PACK),
            )
            return g

        def quantize_w2(e, g):
            words, scales = quantize(g, N, keep, f"w2_{e}")
            w2_q[e] = (words[:], scales[:])

        def silu(a_acc, spent):
            act = spent.rearrange("p (c t) -> p c t", t=PACK)
            nc.scalar.activation(out=act, in_=a_acc[:].rearrange("p t c -> p c t"), func=SILU)
            return act

        def gated(act, b_acc, h_bf):
            nc.vector.tensor_tensor(
                out=h_bf.rearrange("p (c t) -> p c t", t=PACK),
                in0=b_acc[:].rearrange("p t c -> p c t"),
                in1=act,
                op=MULT,
            )

        def quantize_h(e, h_bf):
            h_q[e] = quantize(h_bf, C, keep, f"h_{e}")

        def second_layer(e, acc):
            words, scales = w2_q[e]
            h_words, h_scales = h_q[e]
            nc.tensor.matmul_mx(
                out=acc,
                lhsT=words.bitcast(FP8X4),
                lhsT_scale=scales,
                rhs=h_words[:].bitcast(FP8X4),
                rhs_scale=h_scales[:],
                start=True,
                stop=True,
            )

        w2_q = {}
        h_q = {}
        pos_sb = []
        slots = gather_tokens(0)
        w2_early = keep.tile([P, EARLY, PACK * N], F32, name="w2_early")
        nc.sync.dma_start(out=w2_early[:], in_=w2_view(0, EARLY))
        chunks = []
        for which, w in enumerate((w1, w3)):
            tile = ring_tile([P, PAIRED * PASSES, PACK * H])
            load_passes(tile[:], w, 0, PAIRED * PASSES)
            chunks.extend((which, i // PASSES, i % PASSES, tile[:, i, :]) for i in range(PAIRED * PASSES))
            if which == 0:
                for r, pos in enumerate((pos1, pos2, pos3, pos4)):
                    pos_tile = lists.tile([P, T // LIST_ROWS], U16, name=f"pos_sb{r}")
                    nc.sync.dma_start(pos_tile[:], pos)
                    pos_sb.append(pos_tile)

        def load_expert(e):
            count = 2 * PASSES - (1 if e == E - 1 else 0)
            tile = ring_tile([P, count, PACK * H])
            step = PASSES if e < WHOLE else 1
            for i in range(0, count, step):
                load_passes(tile[:, i : i + step, :], (w1, w3)[i // PASSES], e * PASSES + i % PASSES, step)
            chunks.extend((i // PASSES, e, i % PASSES, tile[:, i, :]) for i in range(count))

        total_chunks = 2 * PASSES * E
        w_q, a_acc, slots_of = {}, {}, {0: slots}
        waiting = []
        for index in range(total_chunks - 1):
            if index == len(chunks):
                load_expert(index // (2 * PASSES))
            which, e, s, rows = chunks[index]
            pair = e // GATHER_EXPERTS
            if pair not in slots_of:
                slots_of[pair] = gather_tokens(e)
            left = total_chunks - 1 - index
            g = cast_shared(rows, LAST_SHARES[-left] if left <= len(LAST_SHARES) else SHARE)
            w_q[which, e, s] = quantize(g[:], H, codes, "w")
            for done, act, b_acc in waiting:
                h_bf = g[:, : C * PACK]
                gated(act, b_acc, h_bf)
                quantize_h(done, h_bf)
                if done < EARLY:
                    w2_bf = small.tile([P, PACK * N], BF16, name="w2_bf", align_bytes=64)
                    quantize_w2(done, cast_w2(w2_early[:, done, :], w2_bf[:]))
                if done == EARLY - 1:
                    y_acc = psum.tile([P, EARLY, C], F32, name="y_acc", tag="y")
                    for i in range(EARLY):
                        second_layer(i, y_acc[:, i, :])
                    nc.scalar.copy(out=y_sb[:, : EARLY * C], in_=y_acc[:].rearrange("p i c -> p (i c)"))
            waiting = []
            cols = slice((e % GATHER_EXPERTS) * C, (e % GATHER_EXPERTS + 1) * C)
            if s == PASSES - 1:
                both = [w_q[which, e, 0], w_q[which, e, 1]]
                acc = project(both, slots_of[pair][0], slots_of[pair][1], cols, ("a_acc", "b_acc")[which])
                if which == 0:
                    a_acc[e] = acc
                else:
                    waiting = [(e, silu(a_acc[e], rows[:, : C * PACK]), acc)]

        act = silu(a_acc[E - 1], rows[:, : C * PACK])
        end_raw = ring_tile([P, 1, PACK * H])
        load_passes(end_raw[:], w3, E * PASSES - 1, 1)
        g = bf_tile(PACK * H)
        nc.vector.tensor_copy(out=permuted(g), in_=columns(end_raw[:, 0, :]))
        b_acc = project([w_q[1, E - 1, 0], quantize_by_tile(g)], slots_of[pair][0], slots_of[pair][1], cols, "b_acc")
        late_bf = bf_tile(LATE * PACK * N)
        late_codes = bf_tile(LATE * N, U32)
        late_scales = keep.tile([P, LATE * N], U8, name="late_scales", align_bytes=64)
        tail = ring_tile([P, LATE * PACK * N + TOP * T])
        late = [late_bf[:, i * PACK * N : (i + 1) * PACK * N] for i in range(LATE)]
        for i in range(LATE):
            rows = tail[:, i * PACK * N : (i + 1) * PACK * N]
            nc.sync.dma_start(out=rows, in_=w2[EARLY + i].rearrange("(p j) n -> p (j n)", j=PACK))
            cast_w2(rows, late[i])

        def quantize_late(i):
            words, scales = late_codes[:, i * N : (i + 1) * N], late_scales[:, i * N : (i + 1) * N]
            nc.vector.quantize_mx(out=words.bitcast(FP8X4), scales=scales, in_=late[i])
            w2_q[EARLY + i] = (words, scales)

        for i in range(LATE - 2):
            quantize_late(i)
        gated(act, b_acc, late[LATE - 3])
        quantize_late(LATE - 2)
        quantize_h(E - 1, late[LATE - 3])
        quantize_late(LATE - 1)
        y_late = psum.tile([P, LATE - 1, C], F32, name="y_late", tag="y")
        for i in range(LATE - 1):
            second_layer(EARLY + i, y_late[:, i, :])
        nc.scalar.copy(out=y_sb[:, EARLY * C : (E - 1) * C], in_=y_late[:].rearrange("p i c -> p (i c)"))
        y_last = psum.tile([P, C], F32, name="y_last", tag="y")
        second_layer(7, y_last[:])
        nc.vector.tensor_copy(out=y_sb[:, 7 * C : 8 * C], in_=y_last[:])

        gates = [tail[:, LATE * PACK * N + r * T : LATE * PACK * N + (r + 1) * T] for r in range(TOP)]
        for r in range(TOP):
            nc.sync.dma_start(out=gates[r], in_=gate[r])
        prods = [keep.tile([P, T], F32, name=f"prod{r}") for r in range(TOP)]

        def weigh(r):
            nc.vector.tensor_tensor(out=prods[r][:], in0=y_sb[:].indirect(pos_sb[r][:]), in1=gates[r], op=MULT)

        sum2 = keep.tile([P, T], F32, name="sum2")
        weigh(0)
        weigh(1)
        weigh(2)
        nc.vector.tensor_tensor(out=sum2[:], in0=prods[0][:], in1=prods[1][:], op=ADD)
        weigh(3)
        token_halves = (slice(0, T // 2), slice(T // 2, T))
        sum3 = [keep.tile([P, T // 2], F32, name=f"sum3_{i}") for i in range(2)]
        total = [keep.tile([P, T // 2], F32, name=f"total{i}") for i in range(2)]
        for i, cols in enumerate(token_halves):
            nc.vector.tensor_tensor(out=sum3[i][:], in0=sum2[:, cols], in1=prods[2][:, cols], op=ADD)
        for i, cols in enumerate(token_halves):
            nc.vector.tensor_tensor(out=total[i][:], in0=sum3[i][:], in1=prods[3][:, cols], op=ADD)
            nc.sync.dma_start(out=out[:, cols], in_=total[i][:])
